import numpy as np
import ml_dtypes


def mxq(x, axis, fmt="e4m3"):
    dtype, down = {"e4m3": (ml_dtypes.float8_e4m3fn, 7), "e5m2": (ml_dtypes.float8_e5m2, 14)}[fmt]
    v = np.moveaxis(np.asarray(x, np.float32).astype(ml_dtypes.bfloat16).astype(np.float64), axis, -1)
    blocks = v.reshape(v.shape[:-1] + (-1, 32))
    amax = np.abs(blocks).max(-1, keepdims=True)
    byte = np.maximum(np.where(amax > 0, np.frexp(amax)[1] - 1 + 127, 0) - down, 1)
    scale = np.exp2(byte - 127.0)
    codes = (blocks / scale).astype(np.float32).astype(dtype).astype(np.float64)
    return np.moveaxis((codes * scale).reshape(v.shape), -1, axis)


WIDE = False


def mx_kscale(k):
    if not WIDE:
        return np.ones(k)
    levels = np.array([10, -10, 5, -5, 0])
    if k % 512:
        return np.exp2(np.random.permutation(np.resize(levels, k // 32))).repeat(32)
    a = np.empty((k // 512, 16))
    for p in range(k // 512):
        a[p, :8] = np.random.permutation(np.resize(levels, 8))
        for g in range(8):
            far = levels[np.abs(levels - a[p, g]) >= 10]
            a[p, g + 8] = far[np.random.randint(len(far))]
    return np.exp2(a.ravel()).repeat(32)


def f64(x):
    return np.asarray(x).astype(np.float64)


def striped(idx):
    return np.tile(idx.reshape(-1, 16).T, (8, 1)).astype(np.uint16)


def unstriped(offs):
    return offs[:16].T.reshape(-1).astype(np.int64)


E2M1 = np.array([0.0, 0.5, 1.0, 1.5, 2.0, 3.0, 4.0, 6.0, -0.0, -0.5, -1.0, -1.5, -2.0, -3.0, -4.0, -6.0])


def pack_weight(w, fmt):
    k, n = w.shape
    w = f64(np.asarray(w, np.float32).astype(ml_dtypes.bfloat16)).reshape(k // 32, 32, n)
    amax = np.abs(w).max(1)
    if fmt == "e4m3":
        byte = np.frexp(amax)[1] - 1 + 127 - 7
    else:
        mant, ex = np.frexp(amax / 6.0)
        byte = np.where(mant > 0.5, ex, ex - 1) + 127
    byte = np.clip(np.where(amax > 0, byte, 1), 1, 254)
    scaled = (w * np.exp2(127.0 - byte)[:, None, :]).reshape(k, n).astype(np.float32)
    by_word = np.ascontiguousarray(scaled.reshape(k // 512, 128, 4, n).transpose(0, 1, 3, 2))
    if fmt == "e4m3":
        words = by_word.astype(ml_dtypes.float8_e4m3fn).view(np.uint8)
    else:
        c = by_word.astype(ml_dtypes.float4_e2m1fn).view(np.uint8) & 0xF
        words = (c[..., 0::2] | (c[..., 1::2] << 4)).reshape(k // 512, 128, 2 * n)
    return np.ascontiguousarray(words), np.ascontiguousarray(byte.astype(np.uint8).reshape(k // 512, 16, n))


def unpack_weight(words, scales, fmt):
    g, _, n = scales.shape
    words = np.ascontiguousarray(words).reshape(g, 128, n, -1)
    if fmt == "e4m3":
        vals = words.view(ml_dtypes.float8_e4m3fn).astype(np.float64)
    else:
        nib = np.empty((g, 128, n, 4), np.uint8)
        nib[..., 0::2] = words & 0xF
        nib[..., 1::2] = words >> 4
        vals = E2M1[nib]
    vals = vals * np.repeat(np.exp2(scales.astype(np.float64) - 127.0), 8, axis=1)[..., None]
    return vals.transpose(0, 1, 3, 2).reshape(g * 512, n)


def gelu(v):
    return 0.5 * v * (1.0 + np.tanh(np.sqrt(2.0 / np.pi) * (v + 0.044715 * v**3)))


K, T, H, S, N = 1024, 2048, 1024, 1024, 512

def setup_inputs():
    n = np.random.standard_normal
    s = mx_kscale(K)[:, None]
    u = mx_kscale(H)[:, None]
    tab_words, tab_scales = pack_weight(n((K, T)) * s, "e4m3")
    tab2_words, tab2_scales = pack_weight(n((K, T)) * s, "e4m3")
    w1 = (n((K, H)) / np.sqrt(K) / s * u.T).astype(np.float32)
    w2 = (n((K, H)) / np.sqrt(K) / s * u.T).astype(np.float32)
    w4_words, w4_scales = pack_weight(n((H, N)) / np.sqrt(H) / u, "e2m1")
    b = (0.5 * n(N)).astype(np.float32)
    return {"tab_words": tab_words, "tab_scales": tab_scales,
            "tab2_words": tab2_words, "tab2_scales": tab2_scales,
            "offs": striped(np.random.permutation(T)[:S]),
            "offs2": striped(np.random.permutation(T)[:S]),
            "w1": w1, "w2": w2, "w4_words": w4_words, "w4_scales": w4_scales, "b": b}

def reference(tab_words, tab_scales, tab2_words, tab2_scales, offs, offs2, w1, w2, w4_words, w4_scales, b):
    v = unpack_weight(tab_words, tab_scales, "e4m3")[:, unstriped(offs)]
    v2 = unpack_weight(tab2_words, tab2_scales, "e4m3")[:, unstriped(offs2)]
    w1q = mxq(f64(w1), 0, "e4m3")
    w2q = mxq(f64(w2), 0, "e4m3")
    w4 = unpack_weight(w4_words, w4_scales, "e2m1")
    gx = w1q.T @ v
    gy = w2q.T @ v2
    h = np.sqrt(np.square(gx) + np.square(gy))
    hq = mxq(h, 0, "e4m3")
    y = w4.T @ hq
    return y + f64(b)[:, None]

@@ -1,0 +1,204 @@
+from contextlib import ExitStack
+
+import concourse.mybir as mybir
+
+K, T, H, S, N = 1024, 2048, 1024, 1024, 512
+FLOPS = 2 * 2 * K * H * S + 2 * H * N * S
+
+F32 = mybir.dt.float32
+BF16 = mybir.dt.bfloat16
+I32 = mybir.dt.int32
+U32 = mybir.dt.uint32
+U16 = mybir.dt.uint16
+U8 = mybir.dt.uint8
+FP8X4 = mybir.dt.float8_e4m3fn_x4
+FP4X4 = mybir.dt.float4_e2m1fn_x4
+ACT = mybir.ActivationFunctionType
+ALU = mybir.AluOpType
+
+P = 128
+PACK = 4
+K_PASS = P * PACK
+HALF = 512
+CH = 256
+
+LOADS = []
+PROGRAM = [["l","w100"],["l","T10"],["l","w110"],["l","T11"],["l","w101"],["s",0,0],["s",0,1],["c",0,0,0],["l","w111"],["g",0,0,0],["q",0,0,0],["g",0,0,1],["l","T20"],["c",0,1,0],["l","w200"],["g",0,1,0],["q",0,1,0],["g",0,1,1],["l","T21"],["m",0,0,0],["m",0,0,1],["m",0,0,2],["m",0,0,3],["c",0,0,1],["l","w210"],["c",0,1,1],["l","w201"],["q",0,0,1],["q",0,1,1],["s",1,0],["s",1,1],["g",1,0,0],["c",1,0,0],["l","w211"],["g",1,1,0],["q",1,0,0],["c",1,1,0],["q",1,1,0],["g",1,0,1],["g",1,1,1],["l","w4"],["m",0,1,0],["m",0,1,1],["m",0,1,2],["m",0,1,3],["m",1,0,0],["a",0,0],["m",1,0,1],["a",0,1],["m",1,0,2],["a",0,2],["m",1,0,3],["a",0,3],["c",1,0,1],["c",1,1,1],["q",1,0,1],["q",1,1,1],["r",0,0],["h",0,0],["r",0,1],["h",0,1],["r",0,2],["h",0,2],["r",0,3],["h",0,3],["m",1,1,0],["a",1,0],["r",1,0],["h",1,0],["o",0,0],["o",0,1],["m",1,1,1],["a",1,1],["r",1,1],["h",1,1],["o",1,0],["o",1,1],["m",1,1,2],["a",1,2],["r",1,2],["h",1,2],["o",2,0],["o",2,1],["m",1,1,3],["a",1,3],["r",1,3],["h",1,3],["o",3,0],["o",3,1]]
+CAST = {"w100":[["A",128]],"w110":[["A",128]],"w101":[["V",128]],"w111":[["V",128]],"w200":[["A",128]],"w210":[["A",128]],"w201":[["V",128]],"w211":[["V",128]]}
+OUT_ENGINE = "VVVVVVVA"
+
+
+def tile_list_gradient_magnitude_descriptors_kernel(
+    tc, tab_words, tab_scales, tab2_words, tab2_scales, offs, offs2, w1, w2, w4_words, w4_scales, b, out
+):
+    nc = tc.nc
+    words_hbm = [tab_words, tab2_words]
+    scales_hbm = [tab_scales, tab2_scales]
+    w_hbm = [w1, w2]
+
+    with ExitStack() as ctx:
+        keep = ctx.enter_context(tc.tile_pool(name="keep", bufs=1))
+        ring = ctx.enter_context(tc.tile_pool(name="ring", bufs=2))
+        psum = ctx.enter_context(tc.psum_pool(name="psum", bufs=8))
+
+        lists = []
+        for d, src in enumerate((offs, offs2)):
+            lst = keep.tile([P, S // 16], U16, name=f"list{d}")
+            nc.sync.dma_start(lst[:], src)
+            lists.append(lst)
+
+        scale_win = []
+        for d in range(2):
+            win = keep.tile([P, T // 4], I32, name=f"scale_win{d}")
+            nc.vector.memset(win[:], 0)
+            rows = scales_hbm[d].bitcast(I32)
+            for q in range(4):
+                nc.scalar.dma_start(win[32 * q : 32 * q + 8, :], rows[:, 4 * q : 4 * q + 4, :])
+            scale_win.append(win)
+
+        one = keep.tile([P, 1], F32, name="one")
+        warm = keep.tile([P, 1], F32, name="warm")
+        nc.vector.memset(one[:], 1.0)
+        nc.scalar.activation(warm[:], one[:], ACT.Sqrt)
+        late = {}
+
+        word_win, w_raw = {}, {}
+
+        def load(name):
+            if name[0] == "T":
+                d, a = int(name[1]) - 1, int(name[2])
+                win = ring.tile([P, T], I32, name="word_win", align_bytes=64, bufs=2)
+                nc.sync.dma_start(win[:], words_hbm[d][a].rearrange("p t i -> p (t i)").bitcast(I32))
+                word_win[d, a] = win
+            elif name == "w4":
+                w4_sb = ring.tile([P, 2, 2 * N], U8, name="raw", align_bytes=64, bufs=3)
+                w4_planes = ring.tile([P, 2, N], U8, name="word_win", align_bytes=64, bufs=2)
+                bias = ring.tile([P, N // P], F32, name="word_win", align_bytes=64, bufs=2)
+                late["words"], late["planes"], late["bias"] = w4_sb, w4_planes, bias
+                nc.gpsimd.memset(w4_planes[:].bitcast(I32), 0)
+                nc.sync.dma_start(w4_sb[:].bitcast(I32), w4_words.bitcast(I32).rearrange("a p c -> p a c"))
+                rows = w4_scales.bitcast(I32)
+                for q in range(4):
+                    nc.sync.dma_start(
+                        w4_planes[32 * q : 32 * q + 4, :, :].bitcast(I32),
+                        rows[:, 4 * q : 4 * q + 4, :].rearrange("a r c -> r a c"),
+                    )
+                with nc.allow_non_contiguous_dma(reason="one bias value to a partition"):
+                    nc.sync.dma_start(bias[:], b.rearrange("(c p) -> p c", p=P))
+            else:
+                d, a, blk = int(name[1]) - 1, int(name[2]), int(name[3])
+                raw = ring.tile([P, PACK, K_PASS], F32, name="raw", align_bytes=64, bufs=3)
+                src = w_hbm[d][a * K_PASS : (a + 1) * K_PASS, blk * K_PASS : (blk + 1) * K_PASS]
+                nc.sync.dma_start(raw[:], src.rearrange("(p i) r -> p i r", i=PACK))
+                w_raw[d, a, blk] = raw
+
+        v_words, v_planes, w_grouped, w_words, w_planes = {}, {}, {}, {}, {}
+        squares, roots, h_words, h_planes = {}, {}, {}, {}
+
+        def gather_scales(d, half):
+            picked = keep.tile([P, HALF], U8, name=f"v_planes{d}{half}", align_bytes=64)
+            cols = slice(half * HALF // 16, (half + 1) * HALF // 16)
+            nc.vector.tensor_copy(picked[:], scale_win[d][:].bitcast(U8).indirect(lists[d][:, cols]))
+            v_planes[d, half] = picked
+
+        def gather_words(d, a, half):
+            picked = keep.tile([P, HALF], U32, name=f"v_words{d}{a}{half}", align_bytes=64)
+            cols = slice(half * HALF // 16, (half + 1) * HALF // 16)
+            nc.vector.tensor_copy(picked[:], word_win[d, a][:].bitcast(U32).indirect(lists[d][:, cols]))
+            v_words[d, a, half] = picked
+
+        def cast(d, a, blk):
+            grouped = ring.tile([P, K_PASS * PACK], BF16, name="w_grouped", align_bytes=64, bufs=3)
+            dst = grouped[:].rearrange("p (t m i) -> p m t i", t=PACK, i=PACK)
+            src = w_raw[d, a, blk][:].rearrange("p i (m t) -> p m t i", t=PACK)
+            lo = 0
+            for engine, count in CAST["w%d%d%d" % (d + 1, a, blk)]:
+                part = slice(lo, lo + count)
+                lo += count
+                if engine == "A":
+                    nc.scalar.copy(dst[:, part], src[:, part])
+                elif engine == "V":
+                    nc.vector.tensor_copy(dst[:, part], src[:, part])
+                else:
+                    nc.gpsimd.tensor_scalar(dst[:, part], src[:, part], 1.0, 0.0, ALU.mult, ALU.add)
+            w_grouped[d, a, blk] = grouped
+
+        def quantize_w(d, a, blk):
+            words = keep.tile([P, K_PASS], U32, name=f"w_words{d}{a}{blk}", align_bytes=64)
+            planes = keep.tile([P, K_PASS], U8, name=f"w_planes{d}{a}{blk}", align_bytes=64)
+            nc.vector.quantize_mx(out=words[:].bitcast(FP8X4), scales=planes[:], in_=w_grouped[d, a, blk][:])
+            w_words[d, a, blk], w_planes[d, a, blk] = words, planes
+
+        def filter_and_square(d, blk, c):
+            half, cols = divmod(c * CH, HALF)
+            cols = slice(cols, cols + CH)
+            if d == 0:
+                sq = keep.tile([P, 2, CH, 2], F32, name=f"gx_sq{blk}{c}")
+            else:
+                sq = ring.tile([P, 2, CH, 2], F32, name="gy_sq", bufs=4)
+            for u in range(2):
+                bank = psum.tile([P, 2, CH], F32, name="bank")
+                for e in range(2):
+                    t = 2 * u + e
+                    m_cols = slice(t * P, (t + 1) * P)
+                    for a in range(2):
+                        nc.tensor.matmul_mx(
+                            out=bank[:, e, :],
+                            lhsT=w_words[d, a, blk][:, m_cols].bitcast(FP8X4),
+                            lhsT_scale=w_planes[d, a, blk][:, m_cols],
+                            rhs=v_words[d, a, half][:, cols].bitcast(FP8X4),
+                            rhs_scale=v_planes[d, half][4 * a : P, cols],
+                            start=(a == 0),
+                            stop=(a == 1),
+                        )
+                nc.scalar.activation(sq[:, u], bank[:].rearrange("p e j -> p j e"), ACT.Square)
+            squares[d, blk, c] = sq
+
+        def add_squares(blk, c):
+            total = squares[0, blk, c]
+            nc.vector.tensor_tensor(total[:], total[:], squares[1, blk, c][:], ALU.add)
+
+        def root(blk, c):
+            mag = ring.tile([P, CH, 2, 2], BF16, name="mag", align_bytes=64, bufs=3)
+            nc.scalar.activation(mag[:], squares[0, blk, c][:].rearrange("p u j e -> p j u e"), ACT.Sqrt)
+            roots[blk, c] = mag
+
+        def quantize_h(blk, c):
+            words = keep.tile([P, CH], U32, name=f"h_words{blk}{c}", align_bytes=64)
+            planes = keep.tile([P, CH], U8, name=f"h_planes{blk}{c}", align_bytes=64)
+            nc.vector.quantize_mx(
+                out=words[:].bitcast(FP8X4), scales=planes[:], in_=roots[blk, c][:].rearrange("p j u e -> p (j u e)")
+            )
+            h_words[blk, c], h_planes[blk, c] = words, planes
+
+        def describe(c, pair):
+            w4_sb, w4_planes, bias = late["words"], late["planes"], late["bias"]
+            bank = psum.tile([P, 2, CH], F32, name="bank")
+            staged = ring.tile([P, 2, CH], F32, name="staged", bufs=4)
+            for i in range(2):
+                n = 2 * pair + i
+                for j0 in range(0, CH, P):
+                    cols = slice(j0, j0 + P)
+                    for blk in range(2):
+                        nc.tensor.matmul_mx(
+                            out=bank[:, i, cols],
+                            lhsT=w4_sb[:, blk, 2 * n * P : 2 * (n + 1) * P].bitcast(FP4X4),
+                            lhsT_scale=w4_planes[:, blk, n * P : (n + 1) * P],
+                            rhs=h_words[blk, c][:, cols].bitcast(FP8X4),
+                            rhs_scale=h_planes[blk, c][:, cols],
+                            start=(blk == 0),
+                            stop=(blk == 1),
+                        )
+            for i in range(2):
+                n = 2 * pair + i
+                if OUT_ENGINE[2 * c + pair] == "A":
+                    nc.scalar.activation(staged[:, i, :], bank[:, i, :], ACT.Identity, bias=bias[:, n : n + 1])
+                else:
+                    nc.vector.tensor_scalar(staged[:, i, :], bank[:, i, :], bias[:, n : n + 1], None, ALU.add)
+            rows = out[2 * pair * P : 2 * (pair + 1) * P, c * CH : (c + 1) * CH]
+            nc.sync.dma_start(rows.rearrange("(i p) j -> p i j", p=P), staged[:])
+
+        steps = {"l": load, "s": gather_scales, "g": gather_words, "c": cast, "q": quantize_w, "m": filter_and_square,
+                 "a": add_squares, "r": root, "h": quantize_h, "o": describe}
+        for step in PROGRAM:
+            steps[step[0]](*step[1:])

@@ -19,13 +19,15 @@ ALU = mybir.AluOpType
 P = 128
 PACK = 4
 K_PASS = P * PACK
-HALF = 512
-CH = 256
+SLOT = 8192
 
-LOADS = []
-PROGRAM = [["l","w100"],["l","T10"],["l","w110"],["l","T11"],["l","w101"],["s",0,0],["s",0,1],["c",0,0,0],["l","w111"],["g",0,0,0],["q",0,0,0],["g",0,0,1],["l","T20"],["c",0,1,0],["l","w200"],["g",0,1,0],["q",0,1,0],["g",0,1,1],["l","T21"],["m",0,0,0],["m",0,0,1],["m",0,0,2],["m",0,0,3],["c",0,0,1],["l","w210"],["c",0,1,1],["l","w201"],["q",0,0,1],["q",0,1,1],["s",1,0],["s",1,1],["g",1,0,0],["c",1,0,0],["l","w211"],["g",1,1,0],["q",1,0,0],["c",1,1,0],["q",1,1,0],["g",1,0,1],["g",1,1,1],["l","w4"],["m",0,1,0],["m",0,1,1],["m",0,1,2],["m",0,1,3],["m",1,0,0],["a",0,0],["m",1,0,1],["a",0,1],["m",1,0,2],["a",0,2],["m",1,0,3],["a",0,3],["c",1,0,1],["c",1,1,1],["q",1,0,1],["q",1,1,1],["r",0,0],["h",0,0],["r",0,1],["h",0,1],["r",0,2],["h",0,2],["r",0,3],["h",0,3],["m",1,1,0],["a",1,0],["r",1,0],["h",1,0],["o",0,0],["o",0,1],["m",1,1,1],["a",1,1],["r",1,1],["h",1,1],["o",1,0],["o",1,1],["m",1,1,2],["a",1,2],["r",1,2],["h",1,2],["o",2,0],["o",2,1],["m",1,1,3],["a",1,3],["r",1,3],["h",1,3],["o",3,0],["o",3,1]]
-CAST = {"w100":[["A",128]],"w110":[["A",128]],"w101":[["V",128]],"w111":[["V",128]],"w200":[["A",128]],"w210":[["A",128]],"w201":[["V",128]],"w211":[["V",128]]}
-OUT_ENGINE = "VVVVVVVA"
+WIDTHS = [256,256,256,128,128]
+CUTS = {"S1":[512,512],"S2":[512,512],"T10":[512,512],"T11":[256,256,512],"T20":[512,512],"T21":[256,256,512]}
+PROGRAM = [["s",0],["x"],["l","w100"],["g","S1",0],["l","T10"],["l","w110"],["c",0,0,0,0],["l","T11"],["g","T11",1],["g","T11",2],["c",0,1,0,0],["l","w200"],["l","T20"],["c",0,1,0,1],["g","T11",0],["l","w210"],["g","T20",0],["c",1,0,0,1],["c",1,1,0,0],["l","T21"],["l","w101"],["l","w111"],["g","S1",1],["g","T21",0],["c",1,0,0,0],["l","w201"],["g","T21",2],["g","T10",1],["q",1,0,0],["l","w211"],["w"],["s",1],["c",0,0,1,0],["c",1,1,1,1],["c",0,0,1,1],["c",1,1,0,1],["g","S2",0],["q",0,0,1],["c",0,0,0,1],["q",0,1,0],["g","T21",1],["q",1,1,0],["g","T10",0],["q",0,0,0],["m",0,0,0],["m",1,0,0],["c",0,1,1,1],["m",0,0,4],["m",0,0,1],["c",1,1,1,0],["c",1,0,1,1],["g","T20",1],["g","S2",1],["a",0,0],["c",0,1,1,0],["m",1,0,3],["q",0,1,1],["m",0,0,2],["m",1,0,1],["m",0,1,2],["m",0,1,3],["m",0,0,3],["m",0,1,0],["q",1,1,1],["m",1,0,4],["m",0,1,1],["c",1,0,1,0],["q",1,0,1],["m",1,1,0],["r",0,0],["a",0,1],["a",1,0],["h",0,0],["m",1,0,2],["m",1,1,1],["a",1,1],["r",1,0],["h",1,0],["m",1,1,2],["r",1,1],["a",0,2],["r",0,1],["a",1,2],["r",0,2],["h",1,1],["h",0,1],["r",1,2],["a",0,3],["o",0,1],["h",0,2],["m",1,1,3],["a",1,3],["r",0,3],["m",1,1,4],["o",0,0],["o",1,1],["r",1,3],["m",0,1,4],["a",1,4],["h",1,2],["h",0,3],["o",1,0],["r",1,4],["h",1,3],["o",2,1],["o",2,0],["h",1,4],["a",0,4],["r",0,4],["h",0,4],["o",3,1],["o",3,0],["o",4,0],["o",4,1]]
+CAST = {"w100":"AA","w110":"VA","w200":"VA","w210":"VV","w101":"VV","w111":"VV","w201":"VV","w211":"VV"}
+ON_SCALAR = []
+GATE = {"100":["w200",0],"101":["w200",4096],"202":["w101",0]}
+OUT_ENGINE = "VVVVAVAVVA"
 
 
 def tile_list_gradient_magnitude_descriptors_kernel(
@@ -35,9 +37,11 @@ def tile_list_gradient_magnitude_descriptors_kernel(
     words_hbm = [tab_words, tab2_words]
     scales_hbm = [tab_scales, tab2_scales]
     w_hbm = [w1, w2]
+    starts = [sum(WIDTHS[:c]) for c in range(len(WIDTHS))]
 
     with ExitStack() as ctx:
         keep = ctx.enter_context(tc.tile_pool(name="keep", bufs=1))
+        stream = ctx.enter_context(tc.tile_pool(name="stream", bufs=1))
         ring = ctx.enter_context(tc.tile_pool(name="ring", bufs=2))
         psum = ctx.enter_context(tc.psum_pool(name="psum", bufs=8))
 
@@ -47,81 +51,93 @@ def tile_list_gradient_magnitude_descriptors_kernel(
             nc.sync.dma_start(lst[:], src)
             lists.append(lst)
 
-        scale_win = []
-        for d in range(2):
+        def warm_up():
+            one = keep.tile([P, 1], F32, name="one")
+            warm = keep.tile([P, 1], F32, name="warm")
+            nc.gpsimd.memset(one[:], 1.0)
+            nc.scalar.activation(warm[:], one[:], ACT.Sqrt)
+
+        scale_win = {}
+
+        def load_scales(d):
             win = keep.tile([P, T // 4], I32, name=f"scale_win{d}")
-            nc.vector.memset(win[:], 0)
+            nc.gpsimd.memset(win[:], 0)
             rows = scales_hbm[d].bitcast(I32)
             for q in range(4):
                 nc.scalar.dma_start(win[32 * q : 32 * q + 8, :], rows[:, 4 * q : 4 * q + 4, :])
-            scale_win.append(win)
+            scale_win[d] = win
 
-        one = keep.tile([P, 1], F32, name="one")
-        warm = keep.tile([P, 1], F32, name="warm")
-        nc.vector.memset(one[:], 1.0)
-        nc.scalar.activation(warm[:], one[:], ACT.Sqrt)
-        late = {}
-
-        word_win, w_raw = {}, {}
+        word_win, w_raw, late = {}, {}, {}
+        loaded = []
 
         def load(name):
+            n = len(loaded)
+            loaded.append(name)
+            offset = n * SLOT
             if name[0] == "T":
                 d, a = int(name[1]) - 1, int(name[2])
-                win = ring.tile([P, T], I32, name="word_win", align_bytes=64, bufs=2)
-                nc.sync.dma_start(win[:], words_hbm[d][a].rearrange("p t i -> p (t i)").bitcast(I32))
+                win = stream.tile([P, T], I32, name=f"word_win{d}{a}", offset=offset)
+                queue = nc.scalar if name in ON_SCALAR else nc.sync
+                queue.dma_start(win[:], words_hbm[d][a].rearrange("p t i -> p (t i)").bitcast(I32))
                 word_win[d, a] = win
-            elif name == "w4":
-                w4_sb = ring.tile([P, 2, 2 * N], U8, name="raw", align_bytes=64, bufs=3)
-                w4_planes = ring.tile([P, 2, N], U8, name="word_win", align_bytes=64, bufs=2)
-                bias = ring.tile([P, N // P], F32, name="word_win", align_bytes=64, bufs=2)
-                late["words"], late["planes"], late["bias"] = w4_sb, w4_planes, bias
-                nc.gpsimd.memset(w4_planes[:].bitcast(I32), 0)
-                nc.sync.dma_start(w4_sb[:].bitcast(I32), w4_words.bitcast(I32).rearrange("a p c -> p a c"))
-                rows = w4_scales.bitcast(I32)
-                for q in range(4):
-                    nc.sync.dma_start(
-                        w4_planes[32 * q : 32 * q + 4, :, :].bitcast(I32),
-                        rows[:, 4 * q : 4 * q + 4, :].rearrange("a r c -> r a c"),
-                    )
-                with nc.allow_non_contiguous_dma(reason="one bias value to a partition"):
-                    nc.sync.dma_start(bias[:], b.rearrange("(c p) -> p c", p=P))
             else:
                 d, a, blk = int(name[1]) - 1, int(name[2]), int(name[3])
-                raw = ring.tile([P, PACK, K_PASS], F32, name="raw", align_bytes=64, bufs=3)
+                raw = stream.tile([P, PACK, K_PASS], F32, name=f"raw{d}{a}{blk}", offset=offset)
                 src = w_hbm[d][a * K_PASS : (a + 1) * K_PASS, blk * K_PASS : (blk + 1) * K_PASS]
                 nc.sync.dma_start(raw[:], src.rearrange("(p i) r -> p i r", i=PACK))
                 w_raw[d, a, blk] = raw
 
-        v_words, v_planes, w_grouped, w_words, w_planes = {}, {}, {}, {}, {}
+        def load_w4():
+            w4_sb = keep.tile([P, 2, 2 * N], U8, name="w4_sb", align_bytes=64)
+            w4_planes = keep.tile([P, 2, N], U8, name="w4_planes", align_bytes=64)
+            bias = keep.tile([P, N // P], F32, name="bias")
+            nc.sync.dma_start(w4_sb[:].bitcast(I32), w4_words.bitcast(I32).rearrange("a p c -> p a c"))
+            with nc.allow_non_contiguous_dma(reason="one bias value to a partition"):
+                nc.sync.dma_start(bias[:], b.rearrange("(c p) -> p c", p=P))
+            nc.gpsimd.memset(w4_planes[:].bitcast(I32), 0)
+            rows = w4_scales.bitcast(I32)
+            for q in range(4):
+                nc.sync.dma_start(
+                    w4_planes[32 * q : 32 * q + 4, :, :].bitcast(I32),
+                    rows[:, 4 * q : 4 * q + 4, :].rearrange("a r c -> r a c"),
+                )
+            late["words"], late["planes"], late["bias"] = w4_sb, w4_planes, bias
+
+        picked, w_grouped, w_words, w_planes = {}, {}, {}, {}
         squares, roots, h_words, h_planes = {}, {}, {}, {}
 
-        def gather_scales(d, half):
-            picked = keep.tile([P, HALF], U8, name=f"v_planes{d}{half}", align_bytes=64)
-            cols = slice(half * HALF // 16, (half + 1) * HALF // 16)
-            nc.vector.tensor_copy(picked[:], scale_win[d][:].bitcast(U8).indirect(lists[d][:, cols]))
-            v_planes[d, half] = picked
+        def gather(key, piece):
+            d = int(key[1]) - 1
+            lo, width = sum(CUTS[key][:piece]), CUTS[key][piece]
+            entries = lists[d][:, lo // 16 : (lo + width) // 16]
+            if key[0] == "S":
+                dst = keep.tile([P, width], U8, name=f"v_{key}_{piece}", align_bytes=64)
+                nc.vector.tensor_copy(dst[:], scale_win[d][:].bitcast(U8).indirect(entries))
+            else:
+                dst = keep.tile([P, width], U32, name=f"v_{key}_{piece}", align_bytes=64)
+                nc.vector.tensor_copy(dst[:], word_win[d, int(key[2])][:].bitcast(U32).indirect(entries))
+            picked[key, piece] = dst
 
-        def gather_words(d, a, half):
-            picked = keep.tile([P, HALF], U32, name=f"v_words{d}{a}{half}", align_bytes=64)
-            cols = slice(half * HALF // 16, (half + 1) * HALF // 16)
-            nc.vector.tensor_copy(picked[:], word_win[d, a][:].bitcast(U32).indirect(lists[d][:, cols]))
-            v_words[d, a, half] = picked
+        def columns(key, c):
+            lo = starts[c]
+            for piece, width in enumerate(CUTS[key]):
+                if lo < width:
+                    return picked[key, piece], slice(lo, lo + WIDTHS[c])
+                lo -= width
 
-        def cast(d, a, blk):
-            grouped = ring.tile([P, K_PASS * PACK], BF16, name="w_grouped", align_bytes=64, bufs=3)
-            dst = grouped[:].rearrange("p (t m i) -> p m t i", t=PACK, i=PACK)
-            src = w_raw[d, a, blk][:].rearrange("p i (m t) -> p m t i", t=PACK)
-            lo = 0
-            for engine, count in CAST["w%d%d%d" % (d + 1, a, blk)]:
-                part = slice(lo, lo + count)
-                lo += count
-                if engine == "A":
-                    nc.scalar.copy(dst[:, part], src[:, part])
-                elif engine == "V":
-                    nc.vector.tensor_copy(dst[:, part], src[:, part])
-                else:
-                    nc.gpsimd.tensor_scalar(dst[:, part], src[:, part], 1.0, 0.0, ALU.mult, ALU.add)
-            w_grouped[d, a, blk] = grouped
+        def cast(d, a, blk, u):
+            if (d, a, blk) not in w_grouped:
+                w_grouped[d, a, blk] = ring.tile([P, K_PASS * PACK], BF16, name="w_grouped", align_bytes=64, bufs=4)
+            half = K_PASS * PACK // 2
+            dst = w_grouped[d, a, blk][:, u * half : (u + 1) * half].rearrange("p (e m i) -> p m i e", e=2, i=PACK)
+            src = w_raw[d, a, blk][:].rearrange("p i (m u e) -> p u m i e", u=2, e=2)[:, u]
+            engine = CAST["w%d%d%d" % (d + 1, a, blk)][u]
+            if engine == "A":
+                nc.scalar.copy(dst, src)
+            elif engine == "V":
+                nc.vector.tensor_copy(dst, src)
+            else:
+                nc.gpsimd.tensor_scalar(dst, src, 1.0, 0.0, ALU.mult, ALU.add)
 
         def quantize_w(d, a, blk):
             words = keep.tile([P, K_PASS], U32, name=f"w_words{d}{a}{blk}", align_bytes=64)
@@ -130,24 +146,32 @@ def tile_list_gradient_magnitude_descriptors_kernel(
             w_words[d, a, blk], w_planes[d, a, blk] = words, planes
 
         def filter_and_square(d, blk, c):
-            half, cols = divmod(c * CH, HALF)
-            cols = slice(cols, cols + CH)
-            if d == 0:
-                sq = keep.tile([P, 2, CH, 2], F32, name=f"gx_sq{blk}{c}")
+            width = WIDTHS[c]
+            banks = width // P
+            per_bank = PACK // banks
+            gate = GATE.get("%d%d%d" % (d + 1, blk, c))
+            if gate:
+                offset = loaded.index(gate[0]) * SLOT + gate[1]
+                sq = stream.tile([P, banks, width, per_bank], F32, name=f"sq{d}{blk}{c}", offset=offset)
+            elif d == 0:
+                sq = keep.tile([P, banks, width, per_bank], F32, name=f"sq{d}{blk}{c}")
             else:
-                sq = ring.tile([P, 2, CH, 2], F32, name="gy_sq", bufs=4)
-            for u in range(2):
-                bank = psum.tile([P, 2, CH], F32, name="bank")
-                for e in range(2):
-                    t = 2 * u + e
+                offset = 2 * blk * SLOT + starts[c] * PACK * 4
+                sq = stream.tile([P, banks, width, per_bank], F32, name=f"sq{d}{blk}{c}", offset=offset)
+            planes, s_cols = columns("S%d" % (d + 1), c)
+            for u in range(banks):
+                bank = psum.tile([P, per_bank, width], F32, name="bank")
+                for e in range(per_bank):
+                    t = per_bank * u + e
                     m_cols = slice(t * P, (t + 1) * P)
                     for a in range(2):
+                        words, cols = columns("T%d%d" % (d + 1, a), c)
                         nc.tensor.matmul_mx(
                             out=bank[:, e, :],
                             lhsT=w_words[d, a, blk][:, m_cols].bitcast(FP8X4),
                             lhsT_scale=w_planes[d, a, blk][:, m_cols],
-                            rhs=v_words[d, a, half][:, cols].bitcast(FP8X4),
-                            rhs_scale=v_planes[d, half][4 * a : P, cols],
+                            rhs=words[:, cols].bitcast(FP8X4),
+                            rhs_scale=planes[4 * a : P, s_cols],
                             start=(a == 0),
                             stop=(a == 1),
                         )
@@ -159,13 +183,15 @@ def tile_list_gradient_magnitude_descriptors_kernel(
             nc.vector.tensor_tensor(total[:], total[:], squares[1, blk, c][:], ALU.add)
 
         def root(blk, c):
-            mag = ring.tile([P, CH, 2, 2], BF16, name="mag", align_bytes=64, bufs=3)
+            width = WIDTHS[c]
+            banks = width // P
+            mag = ring.tile([P, width, banks, PACK // banks], BF16, name="mag", align_bytes=64, bufs=4)
             nc.scalar.activation(mag[:], squares[0, blk, c][:].rearrange("p u j e -> p j u e"), ACT.Sqrt)
             roots[blk, c] = mag
 
         def quantize_h(blk, c):
-            words = keep.tile([P, CH], U32, name=f"h_words{blk}{c}", align_bytes=64)
-            planes = keep.tile([P, CH], U8, name=f"h_planes{blk}{c}", align_bytes=64)
+            words = keep.tile([P, WIDTHS[c]], U32, name=f"h_words{blk}{c}", align_bytes=64)
+            planes = keep.tile([P, WIDTHS[c]], U8, name=f"h_planes{blk}{c}", align_bytes=64)
             nc.vector.quantize_mx(
                 out=words[:].bitcast(FP8X4), scales=planes[:], in_=roots[blk, c][:].rearrange("p j u e -> p (j u e)")
             )
@@ -173,11 +199,12 @@ def tile_list_gradient_magnitude_descriptors_kernel(
 
         def describe(c, pair):
             w4_sb, w4_planes, bias = late["words"], late["planes"], late["bias"]
-            bank = psum.tile([P, 2, CH], F32, name="bank")
-            staged = ring.tile([P, 2, CH], F32, name="staged", bufs=4)
+            width = WIDTHS[c]
+            bank = psum.tile([P, 2, width], F32, name="bank")
+            staged = ring.tile([P, 2, width], F32, name="staged", bufs=4)
             for i in range(2):
                 n = 2 * pair + i
-                for j0 in range(0, CH, P):
+                for j0 in range(0, width, P):
                     cols = slice(j0, j0 + P)
                     for blk in range(2):
                         nc.tensor.matmul_mx(
@@ -195,10 +222,10 @@ def tile_list_gradient_magnitude_descriptors_kernel(
                     nc.scalar.activation(staged[:, i, :], bank[:, i, :], ACT.Identity, bias=bias[:, n : n + 1])
                 else:
                     nc.vector.tensor_scalar(staged[:, i, :], bank[:, i, :], bias[:, n : n + 1], None, ALU.add)
-            rows = out[2 * pair * P : 2 * (pair + 1) * P, c * CH : (c + 1) * CH]
+            rows = out[2 * pair * P : 2 * (pair + 1) * P, starts[c] : starts[c] + width]
             nc.sync.dma_start(rows.rearrange("(i p) j -> p i j", p=P), staged[:])
 
-        steps = {"l": load, "s": gather_scales, "g": gather_words, "c": cast, "q": quantize_w, "m": filter_and_square,
+        steps = {"l": load, "s": load_scales, "x": warm_up, "w": load_w4, "g": gather, "c": cast, "q": quantize_w, "m": filter_and_square,
                  "a": add_squares, "r": root, "h": quantize_h, "o": describe}
         for step in PROGRAM:
             steps[step[0]](*step[1:])

@@ -18,214 +18,232 @@ ALU = mybir.AluOpType
 
 P = 128
 PACK = 4
-K_PASS = P * PACK
-SLOT = 8192
+PASS = P * PACK
+LIST_ROWS = 16
+SCALE_ROWS = 4
 
-WIDTHS = [256,256,256,128,128]
-CUTS = {"S1":[512,512],"S2":[512,512],"T10":[512,512],"T11":[256,256,512],"T20":[512,512],"T21":[256,256,512]}
-PROGRAM = [["s",0],["x"],["l","w100"],["g","S1",0],["l","T10"],["l","w110"],["c",0,0,0,0],["l","T11"],["g","T11",1],["g","T11",2],["c",0,1,0,0],["l","w200"],["l","T20"],["c",0,1,0,1],["g","T11",0],["l","w210"],["g","T20",0],["c",1,0,0,1],["c",1,1,0,0],["l","T21"],["l","w101"],["l","w111"],["g","S1",1],["g","T21",0],["c",1,0,0,0],["l","w201"],["g","T21",2],["g","T10",1],["q",1,0,0],["l","w211"],["w"],["s",1],["c",0,0,1,0],["c",1,1,1,1],["c",0,0,1,1],["c",1,1,0,1],["g","S2",0],["q",0,0,1],["c",0,0,0,1],["q",0,1,0],["g","T21",1],["q",1,1,0],["g","T10",0],["q",0,0,0],["m",0,0,0],["m",1,0,0],["c",0,1,1,1],["m",0,0,4],["m",0,0,1],["c",1,1,1,0],["c",1,0,1,1],["g","T20",1],["g","S2",1],["a",0,0],["c",0,1,1,0],["m",1,0,3],["q",0,1,1],["m",0,0,2],["m",1,0,1],["m",0,1,2],["m",0,1,3],["m",0,0,3],["m",0,1,0],["q",1,1,1],["m",1,0,4],["m",0,1,1],["c",1,0,1,0],["q",1,0,1],["m",1,1,0],["r",0,0],["a",0,1],["a",1,0],["h",0,0],["m",1,0,2],["m",1,1,1],["a",1,1],["r",1,0],["h",1,0],["m",1,1,2],["r",1,1],["a",0,2],["r",0,1],["a",1,2],["r",0,2],["h",1,1],["h",0,1],["r",1,2],["a",0,3],["o",0,1],["h",0,2],["m",1,1,3],["a",1,3],["r",0,3],["m",1,1,4],["o",0,0],["o",1,1],["r",1,3],["m",0,1,4],["a",1,4],["h",1,2],["h",0,3],["o",1,0],["r",1,4],["h",1,3],["o",2,1],["o",2,0],["h",1,4],["a",0,4],["r",0,4],["h",0,4],["o",3,1],["o",3,0],["o",4,0],["o",4,1]]
-CAST = {"w100":"AA","w110":"VA","w200":"VA","w210":"VV","w101":"VV","w111":"VV","w201":"VV","w211":"VV"}
-ON_SCALAR = []
-GATE = {"100":["w200",0],"101":["w200",4096],"202":["w101",0]}
-OUT_ENGINE = "VVVVAVAVVA"
+WIDTHS = [256, 256, 256, 128, 128]
+STARTS = [sum(WIDTHS[:c]) for c in range(len(WIDTHS))]
+
+LOADS = [(0, 0), (0, 0, 0), (0, 1, 0), (0, 1), (1, 0, 0), (1, 0), (1, 1, 0), (1, 1),
+         (0, 0, 1), (0, 1, 1), (1, 0, 1), (1, 1, 1)]
+SLOT = 8192
+GY_SQUARE_SLOTS = (0, 2)
+MAGNITUDE_SLOTS = (7, 10)
+RESULT_SLOTS = (8, 9)
+LATE_GX_SQUARE, LATE_GX_SQUARE_SLOT = (0, 0), 6
+
+LOWER, UPPER, BOTH = slice(0, 1), slice(1, 2), slice(0, 2)
+
+STEPS = [
+    ("gather_words", 0, 0, 0, 1024), ("gather_scales", 0), ("cast", 0, 0, 0, UPPER, "scalar"),
+    ("cast", 0, 0, 0, LOWER, "vector"), ("quantize_filters", 0, 0, 0), ("gather_scales", 1),
+    ("gather_words", 0, 1, 0, 512), ("gather_words", 0, 1, 512, 1024), ("cast", 1, 0, 0, UPPER, "vector"),
+    ("cast", 0, 1, 0, BOTH, "scalar"), ("cast", 1, 0, 0, LOWER, "scalar"), ("quantize_filters", 0, 1, 0),
+    ("gather_words", 1, 0, 0, 1024), ("quantize_filters", 1, 0, 0), ("filter", 0, 0, 2),
+    ("cast", 1, 1, 0, LOWER, "vector"), ("cast", 1, 1, 0, UPPER, "scalar"), ("quantize_filters", 1, 1, 0),
+    ("filter", 0, 0, 0), ("filter", 0, 0, 1), ("gather_words", 1, 1, 0, 256), ("gather_words", 1, 1, 256, 512),
+    ("gather_words", 1, 1, 512, 1024), ("filter", 0, 0, 4), ("filter", 1, 0, 0), ("filter", 1, 0, 1),
+    ("cast", 0, 0, 1, BOTH, "vector"), ("filter", 0, 0, 3), ("add", 0, 0), ("filter", 1, 0, 2),
+    ("quantize_filters", 0, 0, 1), ("root", 0, 0), ("cast", 0, 1, 1, BOTH, "vector"), ("add", 0, 1),
+    ("filter", 1, 0, 3), ("quantize_filters", 0, 1, 1), ("cast", 1, 0, 1, BOTH, "vector"), ("filter", 0, 1, 0),
+    ("filter", 1, 0, 4), ("root", 0, 1), ("add", 0, 2), ("filter", 0, 1, 3), ("cast", 1, 1, 1, BOTH, "vector"),
+    ("root", 0, 2), ("quantize_filters", 1, 0, 1), ("filter", 0, 1, 1), ("quantize_filters", 1, 1, 1), ("add", 0, 3),
+    ("filter", 0, 1, 2), ("quantize_magnitudes", 0, 2), ("quantize_magnitudes", 0, 0), ("quantize_magnitudes", 0, 1),
+    ("filter", 1, 1, 0), ("add", 0, 4), ("filter", 1, 1, 2), ("add", 1, 0), ("root", 1, 0), ("filter", 1, 1, 1),
+    ("add", 1, 2), ("quantize_magnitudes", 1, 0), ("root", 1, 2), ("add", 1, 1), ("filter", 1, 1, 3),
+    ("describe", 0, 1, "vector"), ("root", 1, 1), ("add", 1, 3), ("quantize_magnitudes", 1, 2), ("filter", 1, 1, 4),
+    ("describe", 0, 0, "vector"), ("quantize_magnitudes", 1, 1), ("describe", 2, 0, "vector"), ("filter", 0, 1, 4),
+    ("root", 0, 4), ("add", 1, 4), ("root", 0, 3), ("describe", 1, 0, "vector"), ("root", 1, 3),
+    ("quantize_magnitudes", 0, 3), ("root", 1, 4), ("quantize_magnitudes", 0, 4), ("quantize_magnitudes", 1, 3),
+    ("describe", 2, 1, "scalar"), ("quantize_magnitudes", 1, 4), ("describe", 1, 1, "scalar"),
+    ("describe", 3, 1, "vector"), ("describe", 3, 0, "scalar"), ("describe", 4, 1, "vector"),
+    ("describe", 4, 0, "scalar"),
+]
 
 
 def tile_list_gradient_magnitude_descriptors_kernel(
     tc, tab_words, tab_scales, tab2_words, tab2_scales, offs, offs2, w1, w2, w4_words, w4_scales, b, out
 ):
     nc = tc.nc
-    words_hbm = [tab_words, tab2_words]
-    scales_hbm = [tab_scales, tab2_scales]
-    w_hbm = [w1, w2]
-    starts = [sum(WIDTHS[:c]) for c in range(len(WIDTHS))]
+    table_words, table_scales, filters = (tab_words, tab2_words), (tab_scales, tab2_scales), (w1, w2)
 
     with ExitStack() as ctx:
         keep = ctx.enter_context(tc.tile_pool(name="keep", bufs=1))
         stream = ctx.enter_context(tc.tile_pool(name="stream", bufs=1))
-        ring = ctx.enter_context(tc.tile_pool(name="ring", bufs=2))
+        casts = ctx.enter_context(tc.tile_pool(name="casts", bufs=4))
         psum = ctx.enter_context(tc.psum_pool(name="psum", bufs=8))
 
-        lists = []
-        for d, src in enumerate((offs, offs2)):
-            lst = keep.tile([P, S // 16], U16, name=f"list{d}")
-            nc.sync.dma_start(lst[:], src)
-            lists.append(lst)
+        lists, scale_windows, loaded = {}, {}, {}
+        v_words, v_scales, grouped, w_words, w_scales = {}, {}, {}, {}, {}
+        squares, magnitudes, h_words, h_scales = {}, {}, {}, {}
 
-        def warm_up():
-            one = keep.tile([P, 1], F32, name="one")
-            warm = keep.tile([P, 1], F32, name="warm")
-            nc.gpsimd.memset(one[:], 1.0)
-            nc.scalar.activation(warm[:], one[:], ACT.Sqrt)
+        def load_list(d):
+            entries = keep.tile([P, S // LIST_ROWS], U16, name=f"list{d}")
+            nc.sync.dma_start(entries[:], (offs, offs2)[d])
+            lists[d] = entries
 
-        scale_win = {}
-
-        def load_scales(d):
-            win = keep.tile([P, T // 4], I32, name=f"scale_win{d}")
-            nc.gpsimd.memset(win[:], 0)
-            rows = scales_hbm[d].bitcast(I32)
-            for q in range(4):
-                nc.scalar.dma_start(win[32 * q : 32 * q + 8, :], rows[:, 4 * q : 4 * q + 4, :])
-            scale_win[d] = win
-
-        word_win, w_raw, late = {}, {}, {}
-        loaded = []
-
-        def load(name):
-            n = len(loaded)
-            loaded.append(name)
-            offset = n * SLOT
-            if name[0] == "T":
-                d, a = int(name[1]) - 1, int(name[2])
-                win = stream.tile([P, T], I32, name=f"word_win{d}{a}", offset=offset)
-                queue = nc.scalar if name in ON_SCALAR else nc.sync
-                queue.dma_start(win[:], words_hbm[d][a].rearrange("p t i -> p (t i)").bitcast(I32))
-                word_win[d, a] = win
+        def load_slot(slot):
+            if len(LOADS[slot]) == 2:
+                d, a = LOADS[slot]
+                tile = stream.tile([P, T], I32, name=f"table{d}{a}", offset=slot * SLOT)
+                nc.sync.dma_start(tile[:], table_words[d][a].rearrange("p t i -> p (t i)").bitcast(I32))
             else:
-                d, a, blk = int(name[1]) - 1, int(name[2]), int(name[3])
-                raw = stream.tile([P, PACK, K_PASS], F32, name=f"raw{d}{a}{blk}", offset=offset)
-                src = w_hbm[d][a * K_PASS : (a + 1) * K_PASS, blk * K_PASS : (blk + 1) * K_PASS]
-                nc.sync.dma_start(raw[:], src.rearrange("(p i) r -> p i r", i=PACK))
-                w_raw[d, a, blk] = raw
+                d, a, blk = LOADS[slot]
+                tile = stream.tile([P, PACK, PASS], F32, name=f"filters{d}{a}{blk}", offset=slot * SLOT)
+                rows = filters[d][a * PASS : (a + 1) * PASS, blk * PASS : (blk + 1) * PASS]
+                nc.sync.dma_start(tile[:], rows.rearrange("(p i) r -> p i r", i=PACK))
+            loaded[LOADS[slot]] = tile
 
-        def load_w4():
-            w4_sb = keep.tile([P, 2, 2 * N], U8, name="w4_sb", align_bytes=64)
-            w4_planes = keep.tile([P, 2, N], U8, name="w4_planes", align_bytes=64)
-            bias = keep.tile([P, N // P], F32, name="bias")
-            nc.sync.dma_start(w4_sb[:].bitcast(I32), w4_words.bitcast(I32).rearrange("a p c -> p a c"))
-            with nc.allow_non_contiguous_dma(reason="one bias value to a partition"):
-                nc.sync.dma_start(bias[:], b.rearrange("(c p) -> p c", p=P))
-            nc.gpsimd.memset(w4_planes[:].bitcast(I32), 0)
-            rows = w4_scales.bitcast(I32)
-            for q in range(4):
+        def load_scale_rows(d):
+            window = keep.tile([P, T // 4], I32, name=f"scale_window{d}")
+            nc.gpsimd.memset(window[:], 0)
+            rows = table_scales[d].bitcast(I32)
+            for quad in range(4):
                 nc.sync.dma_start(
-                    w4_planes[32 * q : 32 * q + 4, :, :].bitcast(I32),
-                    rows[:, 4 * q : 4 * q + 4, :].rearrange("a r c -> r a c"),
+                    window[32 * quad : 32 * quad + 2 * SCALE_ROWS, :],
+                    rows[:, SCALE_ROWS * quad : SCALE_ROWS * (quad + 1), :],
                 )
-            late["words"], late["planes"], late["bias"] = w4_sb, w4_planes, bias
+            scale_windows[d] = window
 
-        picked, w_grouped, w_words, w_planes = {}, {}, {}, {}
-        squares, roots, h_words, h_planes = {}, {}, {}, {}
+        def gather_scales(d):
+            picked = keep.tile([P, S], U8, name=f"v_scales{d}", align_bytes=64)
+            nc.vector.tensor_copy(picked[:], scale_windows[d][:].bitcast(U8).indirect(lists[d][:]))
+            v_scales[d] = picked
 
-        def gather(key, piece):
-            d = int(key[1]) - 1
-            lo, width = sum(CUTS[key][:piece]), CUTS[key][piece]
-            entries = lists[d][:, lo // 16 : (lo + width) // 16]
-            if key[0] == "S":
-                dst = keep.tile([P, width], U8, name=f"v_{key}_{piece}", align_bytes=64)
-                nc.vector.tensor_copy(dst[:], scale_win[d][:].bitcast(U8).indirect(entries))
-            else:
-                dst = keep.tile([P, width], U32, name=f"v_{key}_{piece}", align_bytes=64)
-                nc.vector.tensor_copy(dst[:], word_win[d, int(key[2])][:].bitcast(U32).indirect(entries))
-            picked[key, piece] = dst
+        def gather_words(d, a, first, last):
+            picked = keep.tile([P, last - first], U32, name=f"v_words{d}{a}_{first}", align_bytes=64)
+            entries = lists[d][:, first // LIST_ROWS : last // LIST_ROWS]
+            nc.vector.tensor_copy(picked[:], loaded[d, a][:].bitcast(U32).indirect(entries))
+            for c, start in enumerate(STARTS):
+                if first <= start < last:
+                    v_words[d, a, c] = picked[:, start - first : start - first + WIDTHS[c]]
 
-        def columns(key, c):
-            lo = starts[c]
-            for piece, width in enumerate(CUTS[key]):
-                if lo < width:
-                    return picked[key, piece], slice(lo, lo + WIDTHS[c])
-                lo -= width
-
-        def cast(d, a, blk, u):
-            if (d, a, blk) not in w_grouped:
-                w_grouped[d, a, blk] = ring.tile([P, K_PASS * PACK], BF16, name="w_grouped", align_bytes=64, bufs=4)
-            half = K_PASS * PACK // 2
-            dst = w_grouped[d, a, blk][:, u * half : (u + 1) * half].rearrange("p (e m i) -> p m i e", e=2, i=PACK)
-            src = w_raw[d, a, blk][:].rearrange("p i (m u e) -> p u m i e", u=2, e=2)[:, u]
-            engine = CAST["w%d%d%d" % (d + 1, a, blk)][u]
-            if engine == "A":
+        def cast(d, a, blk, part, engine):
+            if (d, a, blk) not in grouped:
+                grouped[d, a, blk] = casts.tile([P, PASS * PACK], BF16, name="grouped", align_bytes=64)
+            dst = grouped[d, a, blk][:].rearrange("p (u e m i) -> p u m i e", u=2, e=2, i=PACK)[:, part]
+            src = loaded[d, a, blk][:].rearrange("p i (m u e) -> p u m i e", u=2, e=2)[:, part]
+            if engine == "scalar":
                 nc.scalar.copy(dst, src)
-            elif engine == "V":
-                nc.vector.tensor_copy(dst, src)
             else:
-                nc.gpsimd.tensor_scalar(dst, src, 1.0, 0.0, ALU.mult, ALU.add)
+                nc.vector.tensor_copy(dst, src)
 
-        def quantize_w(d, a, blk):
-            words = keep.tile([P, K_PASS], U32, name=f"w_words{d}{a}{blk}", align_bytes=64)
-            planes = keep.tile([P, K_PASS], U8, name=f"w_planes{d}{a}{blk}", align_bytes=64)
-            nc.vector.quantize_mx(out=words[:].bitcast(FP8X4), scales=planes[:], in_=w_grouped[d, a, blk][:])
-            w_words[d, a, blk], w_planes[d, a, blk] = words, planes
+        def quantize_filters(d, a, blk):
+            words = keep.tile([P, PASS], U32, name=f"w_words{d}{a}{blk}", align_bytes=64)
+            scales = keep.tile([P, PASS], U8, name=f"w_scales{d}{a}{blk}", align_bytes=64)
+            nc.vector.quantize_mx(out=words[:].bitcast(FP8X4), scales=scales[:], in_=grouped[d, a, blk][:])
+            w_words[d, a, blk], w_scales[d, a, blk] = words, scales
 
         def filter_and_square(d, blk, c):
             width = WIDTHS[c]
             banks = width // P
             per_bank = PACK // banks
-            gate = GATE.get("%d%d%d" % (d + 1, blk, c))
-            if gate:
-                offset = loaded.index(gate[0]) * SLOT + gate[1]
-                sq = stream.tile([P, banks, width, per_bank], F32, name=f"sq{d}{blk}{c}", offset=offset)
-            elif d == 0:
-                sq = keep.tile([P, banks, width, per_bank], F32, name=f"sq{d}{blk}{c}")
+            shape, name = [P, banks, width, per_bank], f"square{d}{blk}{c}"
+            if d == 1:
+                square = stream.tile(shape, F32, name=name, offset=GY_SQUARE_SLOTS[blk] * SLOT + STARTS[c] * PACK * 4)
+            elif (blk, c) == LATE_GX_SQUARE:
+                square = stream.tile(shape, F32, name=name, offset=LATE_GX_SQUARE_SLOT * SLOT)
             else:
-                offset = 2 * blk * SLOT + starts[c] * PACK * 4
-                sq = stream.tile([P, banks, width, per_bank], F32, name=f"sq{d}{blk}{c}", offset=offset)
-            planes, s_cols = columns("S%d" % (d + 1), c)
+                square = keep.tile(shape, F32, name=name)
             for u in range(banks):
                 bank = psum.tile([P, per_bank, width], F32, name="bank")
                 for e in range(per_bank):
                     t = per_bank * u + e
-                    m_cols = slice(t * P, (t + 1) * P)
-                    for a in range(2):
-                        words, cols = columns("T%d%d" % (d + 1, a), c)
+                    for a in range(K // PASS):
                         nc.tensor.matmul_mx(
                             out=bank[:, e, :],
-                            lhsT=w_words[d, a, blk][:, m_cols].bitcast(FP8X4),
-                            lhsT_scale=w_planes[d, a, blk][:, m_cols],
-                            rhs=words[:, cols].bitcast(FP8X4),
-                            rhs_scale=planes[4 * a : P, s_cols],
+                            lhsT=w_words[d, a, blk][:, t * P : (t + 1) * P].bitcast(FP8X4),
+                            lhsT_scale=w_scales[d, a, blk][:, t * P : (t + 1) * P],
+                            rhs=v_words[d, a, c].bitcast(FP8X4),
+                            rhs_scale=v_scales[d][SCALE_ROWS * a : P, STARTS[c] : STARTS[c] + width],
                             start=(a == 0),
-                            stop=(a == 1),
+                            stop=(a == K // PASS - 1),
                         )
-                nc.scalar.activation(sq[:, u], bank[:].rearrange("p e j -> p j e"), ACT.Square)
-            squares[d, blk, c] = sq
+                nc.scalar.activation(square[:, u], bank[:].rearrange("p e j -> p j e"), ACT.Square)
+            squares[d, blk, c] = square
 
         def add_squares(blk, c):
             total = squares[0, blk, c]
             nc.vector.tensor_tensor(total[:], total[:], squares[1, blk, c][:], ALU.add)
 
         def root(blk, c):
-            width = WIDTHS[c]
-            banks = width // P
-            mag = ring.tile([P, width, banks, PACK // banks], BF16, name="mag", align_bytes=64, bufs=4)
-            nc.scalar.activation(mag[:], squares[0, blk, c][:].rearrange("p u j e -> p j u e"), ACT.Sqrt)
-            roots[blk, c] = mag
-
-        def quantize_h(blk, c):
-            words = keep.tile([P, WIDTHS[c]], U32, name=f"h_words{blk}{c}", align_bytes=64)
-            planes = keep.tile([P, WIDTHS[c]], U8, name=f"h_planes{blk}{c}", align_bytes=64)
-            nc.vector.quantize_mx(
-                out=words[:].bitcast(FP8X4), scales=planes[:], in_=roots[blk, c][:].rearrange("p j u e -> p (j u e)")
+            _, banks, width, per_bank = squares[0, blk, c][:].shape
+            magnitude = stream.tile(
+                [P, width, banks, per_bank], BF16, name=f"magnitude{blk}{c}", align_bytes=64,
+                offset=MAGNITUDE_SLOTS[blk] * SLOT + STARTS[c] * PACK * 2,
             )
-            h_words[blk, c], h_planes[blk, c] = words, planes
+            nc.scalar.activation(magnitude[:], squares[0, blk, c][:].rearrange("p u j e -> p j u e"), ACT.Sqrt)
+            magnitudes[blk, c] = magnitude
 
-        def describe(c, pair):
-            w4_sb, w4_planes, bias = late["words"], late["planes"], late["bias"]
+        def quantize_magnitudes(blk, c):
+            words = keep.tile([P, WIDTHS[c]], U32, name=f"h_words{blk}{c}", align_bytes=64)
+            scales = keep.tile([P, WIDTHS[c]], U8, name=f"h_scales{blk}{c}", align_bytes=64)
+            values = magnitudes[blk, c][:].rearrange("p j u e -> p (j u e)")
+            nc.vector.quantize_mx(out=words[:].bitcast(FP8X4), scales=scales[:], in_=values)
+            h_words[blk, c], h_scales[blk, c] = words, scales
+
+        def describe(c, half, engine):
             width = WIDTHS[c]
             bank = psum.tile([P, 2, width], F32, name="bank")
-            staged = ring.tile([P, 2, width], F32, name="staged", bufs=4)
+            result = stream.tile(
+                [P, 2, width], F32, name=f"result{c}{half}", offset=RESULT_SLOTS[half] * SLOT + STARTS[c] * 2 * 4
+            )
             for i in range(2):
-                n = 2 * pair + i
-                for j0 in range(0, width, P):
-                    cols = slice(j0, j0 + P)
-                    for blk in range(2):
+                n = 2 * half + i
+                for j in range(0, width, P):
+                    for blk in range(H // PASS):
                         nc.tensor.matmul_mx(
-                            out=bank[:, i, cols],
-                            lhsT=w4_sb[:, blk, 2 * n * P : 2 * (n + 1) * P].bitcast(FP4X4),
-                            lhsT_scale=w4_planes[:, blk, n * P : (n + 1) * P],
-                            rhs=h_words[blk, c][:, cols].bitcast(FP8X4),
-                            rhs_scale=h_planes[blk, c][:, cols],
+                            out=bank[:, i, j : j + P],
+                            lhsT=w4_codes[:, blk, 2 * n * P : 2 * (n + 1) * P].bitcast(FP4X4),
+                            lhsT_scale=w4_scale_rows[:, blk, n * P : (n + 1) * P],
+                            rhs=h_words[blk, c][:, j : j + P].bitcast(FP8X4),
+                            rhs_scale=h_scales[blk, c][:, j : j + P],
                             start=(blk == 0),
-                            stop=(blk == 1),
+                            stop=(blk == H // PASS - 1),
                         )
-            for i in range(2):
-                n = 2 * pair + i
-                if OUT_ENGINE[2 * c + pair] == "A":
-                    nc.scalar.activation(staged[:, i, :], bank[:, i, :], ACT.Identity, bias=bias[:, n : n + 1])
-                else:
-                    nc.vector.tensor_scalar(staged[:, i, :], bank[:, i, :], bias[:, n : n + 1], None, ALU.add)
-            rows = out[2 * pair * P : 2 * (pair + 1) * P, starts[c] : starts[c] + width]
-            nc.sync.dma_start(rows.rearrange("(i p) j -> p i j", p=P), staged[:])
+            if engine == "scalar":
+                for i in range(2):
+                    n = 2 * half + i
+                    nc.scalar.activation(result[:, i, :], bank[:, i, :], ACT.Identity, bias=bias[:, n : n + 1])
+            else:
+                both = bias[:, 2 * half : 2 * half + 2].unsqueeze(2).to_broadcast([P, 2, width])
+                nc.vector.tensor_tensor(result[:], bank[:], both, ALU.add)
+            rows = out[2 * half * P : 2 * (half + 1) * P, STARTS[c] : STARTS[c] + width]
+            nc.sync.dma_start(rows.rearrange("(i p) j -> p i j", p=P), result[:])
 
-        steps = {"l": load, "s": load_scales, "x": warm_up, "w": load_w4, "g": gather, "c": cast, "q": quantize_w, "m": filter_and_square,
-                 "a": add_squares, "r": root, "h": quantize_h, "o": describe}
-        for step in PROGRAM:
-            steps[step[0]](*step[1:])
+        load_list(0)
+        load_slot(0)
+        load_scale_rows(0)
+
+        one = keep.tile([P, 1], F32, name="one")
+        root_of_one = keep.tile([P, 1], F32, name="root_of_one")
+        nc.gpsimd.memset(one[:], 1.0)
+        nc.scalar.activation(root_of_one[:], one[:], ACT.Sqrt)
+
+        load_slot(1)
+        load_list(1)
+        load_scale_rows(1)
+        for slot in range(2, len(LOADS)):
+            load_slot(slot)
+
+        w4_codes = keep.tile([P, H // PASS, 2 * N], U8, name="w4_codes", align_bytes=64)
+        w4_scale_rows = keep.tile([P, H // PASS, N], U8, name="w4_scale_rows", align_bytes=64)
+        bias = keep.tile([P, N // P], F32, name="bias")
+        nc.sync.dma_start(w4_codes[:].bitcast(I32), w4_words.bitcast(I32).rearrange("a p c -> p a c"))
+        with nc.allow_non_contiguous_dma(reason="one bias value to a partition"):
+            nc.sync.dma_start(bias[:], b.rearrange("(c p) -> p c", p=P))
+        nc.gpsimd.memset(w4_scale_rows[:].bitcast(I32), 0)
+        for quad in range(4):
+            nc.sync.dma_start(
+                w4_scale_rows[32 * quad : 32 * quad + SCALE_ROWS, :, :].bitcast(I32),
+                w4_scales.bitcast(I32)[:, SCALE_ROWS * quad : SCALE_ROWS * (quad + 1), :].rearrange("a r c -> r a c"),
+            )
+
+        actions = {
+            "gather_scales": gather_scales, "gather_words": gather_words, "cast": cast,
+            "quantize_filters": quantize_filters, "filter": filter_and_square, "add": add_squares, "root": root,
+            "quantize_magnitudes": quantize_magnitudes, "describe": describe,
+        }
+        for action, *arguments in STEPS:
+            actions[action](*arguments)

from contextlib import ExitStack

import concourse.mybir as mybir

K, T, H, S, N = 1024, 2048, 1024, 1024, 512
FLOPS = 2 * 2 * K * H * S + 2 * H * N * S

F32 = mybir.dt.float32
BF16 = mybir.dt.bfloat16
I32 = mybir.dt.int32
U32 = mybir.dt.uint32
U16 = mybir.dt.uint16
U8 = mybir.dt.uint8
FP8X4 = mybir.dt.float8_e4m3fn_x4
FP4X4 = mybir.dt.float4_e2m1fn_x4
ACT = mybir.ActivationFunctionType
ALU = mybir.AluOpType

P = 128
PACK = 4
PASS = P * PACK
LIST_ROWS = 16
SCALE_ROWS = 4

WIDTHS = [256, 256, 256, 128, 128]
STARTS = [sum(WIDTHS[:c]) for c in range(len(WIDTHS))]

LOADS = [(0, 0), (0, 0, 0), (0, 1, 0), (0, 1), (1, 0, 0), (1, 0), (1, 1, 0), (1, 1),
         (0, 0, 1), (0, 1, 1), (1, 0, 1), (1, 1, 1)]
SLOT = 8192
GY_SQUARE_SLOTS = (0, 2)
MAGNITUDE_SLOTS = (7, 10)
RESULT_SLOTS = (8, 9)
LATE_GX_SQUARE, LATE_GX_SQUARE_SLOT = (0, 0), 6

LOWER, UPPER, BOTH = slice(0, 1), slice(1, 2), slice(0, 2)

STEPS = [
    ("gather_words", 0, 0, 0, 1024), ("gather_scales", 0), ("cast", 0, 0, 0, UPPER, "scalar"),
    ("cast", 0, 0, 0, LOWER, "vector"), ("quantize_filters", 0, 0, 0), ("gather_scales", 1),
    ("gather_words", 0, 1, 0, 512), ("gather_words", 0, 1, 512, 1024), ("cast", 1, 0, 0, UPPER, "vector"),
    ("cast", 0, 1, 0, BOTH, "scalar"), ("cast", 1, 0, 0, LOWER, "scalar"), ("quantize_filters", 0, 1, 0),
    ("gather_words", 1, 0, 0, 1024), ("quantize_filters", 1, 0, 0), ("filter", 0, 0, 2),
    ("cast", 1, 1, 0, LOWER, "vector"), ("cast", 1, 1, 0, UPPER, "scalar"), ("quantize_filters", 1, 1, 0),
    ("filter", 0, 0, 0), ("filter", 0, 0, 1), ("gather_words", 1, 1, 0, 256), ("gather_words", 1, 1, 256, 512),
    ("gather_words", 1, 1, 512, 1024), ("filter", 0, 0, 4), ("filter", 1, 0, 0), ("filter", 1, 0, 1),
    ("cast", 0, 0, 1, BOTH, "vector"), ("filter", 0, 0, 3), ("add", 0, 0), ("filter", 1, 0, 2),
    ("quantize_filters", 0, 0, 1), ("root", 0, 0), ("cast", 0, 1, 1, BOTH, "vector"), ("add", 0, 1),
    ("filter", 1, 0, 3), ("quantize_filters", 0, 1, 1), ("cast", 1, 0, 1, BOTH, "vector"), ("filter", 0, 1, 0),
    ("filter", 1, 0, 4), ("root", 0, 1), ("add", 0, 2), ("filter", 0, 1, 3), ("cast", 1, 1, 1, BOTH, "vector"),
    ("root", 0, 2), ("quantize_filters", 1, 0, 1), ("filter", 0, 1, 1), ("quantize_filters", 1, 1, 1), ("add", 0, 3),
    ("filter", 0, 1, 2), ("quantize_magnitudes", 0, 2), ("quantize_magnitudes", 0, 0), ("quantize_magnitudes", 0, 1),
    ("filter", 1, 1, 0), ("add", 0, 4), ("filter", 1, 1, 2), ("add", 1, 0), ("root", 1, 0), ("filter", 1, 1, 1),
    ("add", 1, 2), ("quantize_magnitudes", 1, 0), ("root", 1, 2), ("add", 1, 1), ("filter", 1, 1, 3),
    ("describe", 0, 1, "vector"), ("root", 1, 1), ("add", 1, 3), ("quantize_magnitudes", 1, 2), ("filter", 1, 1, 4),
    ("describe", 0, 0, "vector"), ("quantize_magnitudes", 1, 1), ("describe", 2, 0, "vector"), ("filter", 0, 1, 4),
    ("root", 0, 4), ("add", 1, 4), ("root", 0, 3), ("describe", 1, 0, "vector"), ("root", 1, 3),
    ("quantize_magnitudes", 0, 3), ("root", 1, 4), ("quantize_magnitudes", 0, 4), ("quantize_magnitudes", 1, 3),
    ("describe", 2, 1, "scalar"), ("quantize_magnitudes", 1, 4), ("describe", 1, 1, "scalar"),
    ("describe", 3, 1, "vector"), ("describe", 3, 0, "scalar"), ("describe", 4, 1, "vector"),
    ("describe", 4, 0, "scalar"),
]


def tile_list_gradient_magnitude_descriptors_kernel(
    tc, tab_words, tab_scales, tab2_words, tab2_scales, offs, offs2, w1, w2, w4_words, w4_scales, b, out
):
    nc = tc.nc
    table_words, table_scales, filters = (tab_words, tab2_words), (tab_scales, tab2_scales), (w1, w2)

    with ExitStack() as ctx:
        keep = ctx.enter_context(tc.tile_pool(name="keep", bufs=1))
        stream = ctx.enter_context(tc.tile_pool(name="stream", bufs=1))
        casts = ctx.enter_context(tc.tile_pool(name="casts", bufs=4))
        psum = ctx.enter_context(tc.psum_pool(name="psum", bufs=8))

        lists, scale_windows, loaded = {}, {}, {}
        v_words, v_scales, grouped, w_words, w_scales = {}, {}, {}, {}, {}
        squares, magnitudes, h_words, h_scales = {}, {}, {}, {}

        def load_list(d):
            entries = keep.tile([P, S // LIST_ROWS], U16, name=f"list{d}")
            nc.sync.dma_start(entries[:], (offs, offs2)[d])
            lists[d] = entries

        def load_slot(slot):
            if len(LOADS[slot]) == 2:
                d, a = LOADS[slot]
                tile = stream.tile([P, T], I32, name=f"table{d}{a}", offset=slot * SLOT)
                nc.sync.dma_start(tile[:], table_words[d][a].rearrange("p t i -> p (t i)").bitcast(I32))
            else:
                d, a, blk = LOADS[slot]
                tile = stream.tile([P, PACK, PASS], F32, name=f"filters{d}{a}{blk}", offset=slot * SLOT)
                rows = filters[d][a * PASS : (a + 1) * PASS, blk * PASS : (blk + 1) * PASS]
                nc.sync.dma_start(tile[:], rows.rearrange("(p i) r -> p i r", i=PACK))
            loaded[LOADS[slot]] = tile

        def load_scale_rows(d):
            window = keep.tile([P, T // 4], I32, name=f"scale_window{d}")
            nc.gpsimd.memset(window[:], 0)
            rows = table_scales[d].bitcast(I32)
            for quad in range(4):
                nc.sync.dma_start(
                    window[32 * quad : 32 * quad + 2 * SCALE_ROWS, :],
                    rows[:, SCALE_ROWS * quad : SCALE_ROWS * (quad + 1), :],
                )
            scale_windows[d] = window

        def gather_scales(d):
            picked = keep.tile([P, S], U8, name=f"v_scales{d}", align_bytes=64)
            nc.vector.tensor_copy(picked[:], scale_windows[d][:].bitcast(U8).indirect(lists[d][:]))
            v_scales[d] = picked

        def gather_words(d, a, first, last):
            picked = keep.tile([P, last - first], U32, name=f"v_words{d}{a}_{first}", align_bytes=64)
            entries = lists[d][:, first // LIST_ROWS : last // LIST_ROWS]
            nc.vector.tensor_copy(picked[:], loaded[d, a][:].bitcast(U32).indirect(entries))
            for c, start in enumerate(STARTS):
                if first <= start < last:
                    v_words[d, a, c] = picked[:, start - first : start - first + WIDTHS[c]]

        def cast(d, a, blk, part, engine):
            if (d, a, blk) not in grouped:
                grouped[d, a, blk] = casts.tile([P, PASS * PACK], BF16, name="grouped", align_bytes=64)
            dst = grouped[d, a, blk][:].rearrange("p (u e m i) -> p u m i e", u=2, e=2, i=PACK)[:, part]
            src = loaded[d, a, blk][:].rearrange("p i (m u e) -> p u m i e", u=2, e=2)[:, part]
            if engine == "scalar":
                nc.scalar.copy(dst, src)
            else:
                nc.vector.tensor_copy(dst, src)

        def quantize_filters(d, a, blk):
            words = keep.tile([P, PASS], U32, name=f"w_words{d}{a}{blk}", align_bytes=64)
            scales = keep.tile([P, PASS], U8, name=f"w_scales{d}{a}{blk}", align_bytes=64)
            nc.vector.quantize_mx(out=words[:].bitcast(FP8X4), scales=scales[:], in_=grouped[d, a, blk][:])
            w_words[d, a, blk], w_scales[d, a, blk] = words, scales

        def filter_and_square(d, blk, c):
            width = WIDTHS[c]
            banks = width // P
            per_bank = PACK // banks
            shape, name = [P, banks, width, per_bank], f"square{d}{blk}{c}"
            if d == 1:
                square = stream.tile(shape, F32, name=name, offset=GY_SQUARE_SLOTS[blk] * SLOT + STARTS[c] * PACK * 4)
            elif (blk, c) == LATE_GX_SQUARE:
                square = stream.tile(shape, F32, name=name, offset=LATE_GX_SQUARE_SLOT * SLOT)
            else:
                square = keep.tile(shape, F32, name=name)
            for u in range(banks):
                bank = psum.tile([P, per_bank, width], F32, name="bank")
                for e in range(per_bank):
                    t = per_bank * u + e
                    for a in range(K // PASS):
                        nc.tensor.matmul_mx(
                            out=bank[:, e, :],
                            lhsT=w_words[d, a, blk][:, t * P : (t + 1) * P].bitcast(FP8X4),
                            lhsT_scale=w_scales[d, a, blk][:, t * P : (t + 1) * P],
                            rhs=v_words[d, a, c].bitcast(FP8X4),
                            rhs_scale=v_scales[d][SCALE_ROWS * a : P, STARTS[c] : STARTS[c] + width],
                            start=(a == 0),
                            stop=(a == K // PASS - 1),
                        )
                nc.scalar.activation(square[:, u], bank[:].rearrange("p e j -> p j e"), ACT.Square)
            squares[d, blk, c] = square

        def add_squares(blk, c):
            total = squares[0, blk, c]
            nc.vector.tensor_tensor(total[:], total[:], squares[1, blk, c][:], ALU.add)

        def root(blk, c):
            _, banks, width, per_bank = squares[0, blk, c][:].shape
            magnitude = stream.tile(
                [P, width, banks, per_bank], BF16, name=f"magnitude{blk}{c}", align_bytes=64,
                offset=MAGNITUDE_SLOTS[blk] * SLOT + STARTS[c] * PACK * 2,
            )
            nc.scalar.activation(magnitude[:], squares[0, blk, c][:].rearrange("p u j e -> p j u e"), ACT.Sqrt)
            magnitudes[blk, c] = magnitude

        def quantize_magnitudes(blk, c):
            words = keep.tile([P, WIDTHS[c]], U32, name=f"h_words{blk}{c}", align_bytes=64)
            scales = keep.tile([P, WIDTHS[c]], U8, name=f"h_scales{blk}{c}", align_bytes=64)
            values = magnitudes[blk, c][:].rearrange("p j u e -> p (j u e)")
            nc.vector.quantize_mx(out=words[:].bitcast(FP8X4), scales=scales[:], in_=values)
            h_words[blk, c], h_scales[blk, c] = words, scales

        def describe(c, half, engine):
            width = WIDTHS[c]
            bank = psum.tile([P, 2, width], F32, name="bank")
            result = stream.tile(
                [P, 2, width], F32, name=f"result{c}{half}", offset=RESULT_SLOTS[half] * SLOT + STARTS[c] * 2 * 4
            )
            for i in range(2):
                n = 2 * half + i
                for j in range(0, width, P):
                    for blk in range(H // PASS):
                        nc.tensor.matmul_mx(
                            out=bank[:, i, j : j + P],
                            lhsT=w4_codes[:, blk, 2 * n * P : 2 * (n + 1) * P].bitcast(FP4X4),
                            lhsT_scale=w4_scale_rows[:, blk, n * P : (n + 1) * P],
                            rhs=h_words[blk, c][:, j : j + P].bitcast(FP8X4),
                            rhs_scale=h_scales[blk, c][:, j : j + P],
                            start=(blk == 0),
                            stop=(blk == H // PASS - 1),
                        )
            if engine == "scalar":
                for i in range(2):
                    n = 2 * half + i
                    nc.scalar.activation(result[:, i, :], bank[:, i, :], ACT.Identity, bias=bias[:, n : n + 1])
            else:
                both = bias[:, 2 * half : 2 * half + 2].unsqueeze(2).to_broadcast([P, 2, width])
                nc.vector.tensor_tensor(result[:], bank[:], both, ALU.add)
            rows = out[2 * half * P : 2 * (half + 1) * P, STARTS[c] : STARTS[c] + width]
            nc.sync.dma_start(rows.rearrange("(i p) j -> p i j", p=P), result[:])

        load_list(0)
        load_slot(0)
        load_scale_rows(0)

        one = keep.tile([P, 1], F32, name="one")
        root_of_one = keep.tile([P, 1], F32, name="root_of_one")
        nc.gpsimd.memset(one[:], 1.0)
        nc.scalar.activation(root_of_one[:], one[:], ACT.Sqrt)

        load_slot(1)
        load_list(1)
        load_scale_rows(1)
        for slot in range(2, len(LOADS)):
            load_slot(slot)

        w4_codes = keep.tile([P, H // PASS, 2 * N], U8, name="w4_codes", align_bytes=64)
        w4_scale_rows = keep.tile([P, H // PASS, N], U8, name="w4_scale_rows", align_bytes=64)
        bias = keep.tile([P, N // P], F32, name="bias")
        nc.sync.dma_start(w4_codes[:].bitcast(I32), w4_words.bitcast(I32).rearrange("a p c -> p a c"))
        with nc.allow_non_contiguous_dma(reason="one bias value to a partition"):
            nc.sync.dma_start(bias[:], b.rearrange("(c p) -> p c", p=P))
        nc.gpsimd.memset(w4_scale_rows[:].bitcast(I32), 0)
        for quad in range(4):
            nc.sync.dma_start(
                w4_scale_rows[32 * quad : 32 * quad + SCALE_ROWS, :, :].bitcast(I32),
                w4_scales.bitcast(I32)[:, SCALE_ROWS * quad : SCALE_ROWS * (quad + 1), :].rearrange("a r c -> r a c"),
            )

        actions = {
            "gather_scales": gather_scales, "gather_words": gather_words, "cast": cast,
            "quantize_filters": quantize_filters, "filter": filter_and_square, "add": add_squares, "root": root,
            "quantize_magnitudes": quantize_magnitudes, "describe": describe,
        }
        for action, *arguments in STEPS:
            actions[action](*arguments)
